import numpy as np, ml_dtypes
CORES = [129,145,193,257,273,321,385,401,449]
N = 9
F = 128
def setup_inputs(rng):
    return {"a": rng.standard_normal((N, 128, 128), dtype=np.float32).astype(ml_dtypes.bfloat16), "b": rng.standard_normal((N, 128, F), dtype=np.float32).astype(ml_dtypes.bfloat16)}
def setup_inputs_big(rng):
    d = setup_inputs(rng)
    for k in ("a", "b"): d[k] = (d[k].astype(np.float32) * 1024.0).astype(d[k].dtype)
    return d
def setup_inputs_small(rng):
    d = setup_inputs(rng)
    for k in ("a", "b"): d[k] = (d[k].astype(np.float32) * (1 / 1024.0)).astype(d[k].dtype)
    return d
def setup_inputs_apart(rng):
    d = setup_inputs(rng)
    f = (10.0 ** rng.permutation(np.linspace(-1.5, 1.5, N))).astype(np.float32).reshape(N, 1, 1)
    for k in ("a", "b"): d[k] = (d[k].astype(np.float32) * f).astype(d[k].dtype)
    return d
def reference(a, b):
    s = (a.astype(np.float64).sum(axis=0).T @ b.astype(np.float64).sum(axis=0)).astype(ml_dtypes.bfloat16 if a.dtype != np.float64 else np.float64)
    return {"y": np.broadcast_to(s, (N,) + s.shape)}

@@ -1,0 +1,99 @@
+from concourse.bass import DstId, RemoteDMATransfer
+
+R = 8
+UW = 32
+NR = 9
+
+SCRATCH = {
+    "src": ("dram", [R * 128, UW], "bfloat16"),
+    "land": ("dram", [NR * 128, UW], "bfloat16"),
+    "res": ("dram", [R * 128, UW], "bfloat16"),
+    "ab": ("sbuf", [128, 256], "bfloat16"),
+    "ysb": ("sbuf", [128, 128], "bfloat16"),
+    "ps": ("psum", [128, 128], "float32"),
+}
+SEMAPHORES = ["ld", "snt", "arr", "got", "ld2", "mm", "cp", "st"]
+
+
+def _engines(topo, src, dsts):
+    m = topo.mask(src, dsts[0])
+    for d in dsts[1:]:
+        m &= topo.mask(src, d)
+    return [1 << i for i in range(m.bit_length()) if (m >> i) & 1]
+
+
+def _reducers(T, topo):
+    ranks = list(T.cores)
+    per = topo.CORES_PER_HOST
+    chips = {}
+    for h in sorted(set(topo.host(r) for r in ranks)):
+        for c in range(h * per, (h + 1) * per):
+            if c in ranks:
+                continue
+            if all(topo.may_write(r, c) and topo.may_write(c, r) for r in ranks):
+                chips.setdefault((topo.host(c), topo.chip(c)), []).append(c)
+    out = []
+    for k, key in enumerate(sorted(chips)[:R]):
+        dies = sorted(set(topo.die(c) for c in chips[key]))
+        mine = [c for c in chips[key] if topo.die(c) == dies[k % len(dies)]]
+        out.append(mine[(k // len(dies)) % len(mine)])
+    return out
+
+
+def _fold_engines(topo, red_core, ranks):
+    return _engines(topo, red_core, ranks)[0::2]
+
+
+def _unit(t, k):
+    return t[k * 128:(k + 1) * 128, :]
+
+
+def rank_program(g, core, T, topo):
+    ranks = list(T.cores)
+    red = _reducers(T, topo)
+    rank = T.rank_of(core)
+    S = T.sem
+
+    if rank is None:
+        if core not in red:
+            return
+        k = red.index(core)
+        eng = _fold_engines(topo, core, ranks)
+        ids = []
+        for r in ranks:
+            rid, pid = topo.addr(r, core)
+            ids.append(DstId(rid=rid, pnc=pid))
+        g.wait_ge(S.arr, NR)
+        g.remote_dma_fused([RemoteDMATransfer(
+            dst_ids=ids, dma_engine_mask=sum(eng), remote_sem=S.got,
+            srcs=[_unit(T.land, i) for i in range(NR)],
+            dsts=[_unit(T.res, k) for _ in ranks], alu_op=1)], local_sem=S.snt)
+        g.wait_ge(S.snt, len(eng))
+        return
+
+    half = R * 128 // 2
+    g.sync.dma_start(T.src[0:half, :], T.a[:, :]).then_inc(S.ld, 16)
+    g.scalar.dma_start(T.src[half:2 * half, :], T.b[:, :]).then_inc(S.ld, 16)
+    eng = _engines(topo, core, red)
+    trs = []
+    for k, h in enumerate(red):
+        rid, pid = topo.addr(h, core)
+        trs.append(RemoteDMATransfer(
+            dst_ids=[DstId(rid=rid, pnc=pid)], dma_engine_mask=eng[k], remote_sem=S.arr,
+            src=_unit(T.src, k), dst=_unit(T.land, rank)))
+    g.wait_ge(S.ld, 32)
+    g.remote_dma_fused(trs, local_sem=S.snt)
+
+    total = sum(len(_fold_engines(topo, h, ranks)) for h in red)
+    g.sync.wait_ge(S.got, total)
+    g.sync.dma_start(T.ab[:, 0:128], T.res[0:half, :]).then_inc(S.ld2, 16)
+    g.scalar.wait_ge(S.got, total)
+    g.scalar.dma_start(T.ab[:, 128:256], T.res[half:2 * half, :]).then_inc(S.ld2, 16)
+    g.tensor.wait_ge(S.ld2, 32)
+    g.tensor.matmul(T.ps[:, :], T.ab[:, 0:128], T.ab[:, 128:256], True, True).then_inc(S.mm, 1)
+    g.vector.wait_ge(S.mm, 1)
+    g.vector.tensor_copy(T.ysb[:, :], T.ps[:, :]).then_inc(S.cp, 1)
+    g.sync.wait_ge(S.cp, 1)
+    g.sync.dma_start(T.y[:, :], T.ysb[:, :]).then_inc(S.st, 16)
+    g.sync.wait_ge(S.st, 16)
+    g.wait_ge(S.snt, R)

@@ -1,7 +1,7 @@
 from concourse.bass import DstId, RemoteDMATransfer
 
-R = 8
-UW = 32
+R = 16
+UW = 256 // R
 NR = 9
 
 SCRATCH = {
@@ -32,16 +32,15 @@ def _reducers(T, topo):
                 continue
             if all(topo.may_write(r, c) and topo.may_write(c, r) for r in ranks):
                 chips.setdefault((topo.host(c), topo.chip(c)), []).append(c)
+    keys = sorted(chips)
     out = []
-    for k, key in enumerate(sorted(chips)[:R]):
-        dies = sorted(set(topo.die(c) for c in chips[key]))
-        mine = [c for c in chips[key] if topo.die(c) == dies[k % len(dies)]]
-        out.append(mine[(k // len(dies)) % len(mine)])
+    for k in range(R):
+        j, turn = k % len(keys), k // len(keys)
+        cs = chips[keys[j]]
+        dies = sorted(set(topo.die(c) for c in cs))
+        mine = [c for c in cs if topo.die(c) == dies[(j + turn) % len(dies)]]
+        out.append(mine[(j // len(dies)) % len(mine)])
     return out
-
-
-def _fold_engines(topo, red_core, ranks):
-    return _engines(topo, red_core, ranks)[0::2]
 
 
 def _unit(t, k):
@@ -58,7 +57,7 @@ def rank_program(g, core, T, topo):
         if core not in red:
             return
         k = red.index(core)
-        eng = _fold_engines(topo, core, ranks)
+        eng = _engines(topo, core, ranks)
         ids = []
         for r in ranks:
             rid, pid = topo.addr(r, core)
@@ -75,16 +74,17 @@ def rank_program(g, core, T, topo):
     g.sync.dma_start(T.src[0:half, :], T.a[:, :]).then_inc(S.ld, 16)
     g.scalar.dma_start(T.src[half:2 * half, :], T.b[:, :]).then_inc(S.ld, 16)
     eng = _engines(topo, core, red)
-    trs = []
-    for k, h in enumerate(red):
-        rid, pid = topo.addr(h, core)
-        trs.append(RemoteDMATransfer(
-            dst_ids=[DstId(rid=rid, pnc=pid)], dma_engine_mask=eng[k], remote_sem=S.arr,
-            src=_unit(T.src, k), dst=_unit(T.land, rank)))
     g.wait_ge(S.ld, 32)
-    g.remote_dma_fused(trs, local_sem=S.snt)
+    for k0 in range(0, R, len(eng)):
+        trs = []
+        for k in range(k0, min(R, k0 + len(eng))):
+            rid, pid = topo.addr(red[k], core)
+            trs.append(RemoteDMATransfer(
+                dst_ids=[DstId(rid=rid, pnc=pid)], dma_engine_mask=eng[k - k0], remote_sem=S.arr,
+                src=_unit(T.src, k), dst=_unit(T.land, rank)))
+        g.remote_dma_fused(trs, local_sem=S.snt)
 
-    total = sum(len(_fold_engines(topo, h, ranks)) for h in red)
+    total = sum(len(_engines(topo, h, ranks)) for h in red)
     g.sync.wait_ge(S.got, total)
     g.sync.dma_start(T.ab[:, 0:128], T.res[0:half, :]).then_inc(S.ld2, 16)
     g.scalar.wait_ge(S.got, total)

@@ -1,18 +1,21 @@
 from concourse.bass import DstId, RemoteDMATransfer
 
-R = 16
-UW = 256 // R
+G = 4
 NR = 9
+GE = 2 * 128 * 128 // G
 
+SEMAPHORES = (["ld%d" % q for q in range(G)] + ["got%d" % q for q in range(G)]
+              + ["lx0", "lx1", "snt", "arr", "m1", "mm", "cp", "st"])
+U = 8
+UW = GE // U // 128
 SCRATCH = {
-    "src": ("dram", [R * 128, UW], "bfloat16"),
+    "src": ("dram", [G * U * 128, UW], "bfloat16"),
     "land": ("dram", [NR * 128, UW], "bfloat16"),
-    "res": ("dram", [R * 128, UW], "bfloat16"),
+    "res": ("dram", [G * U * 128, UW], "bfloat16"),
     "ab": ("sbuf", [128, 256], "bfloat16"),
     "ysb": ("sbuf", [128, 128], "bfloat16"),
     "ps": ("psum", [128, 128], "float32"),
 }
-SEMAPHORES = ["ld", "snt", "arr", "got", "ld2", "mm", "cp", "st"]
 
 
 def _engines(topo, src, dsts):
@@ -34,17 +37,21 @@ def _reducers(T, topo):
                 chips.setdefault((topo.host(c), topo.chip(c)), []).append(c)
     keys = sorted(chips)
     out = []
-    for k in range(R):
+    for k in range(G * U):
         j, turn = k % len(keys), k // len(keys)
         cs = chips[keys[j]]
         dies = sorted(set(topo.die(c) for c in cs))
         mine = [c for c in cs if topo.die(c) == dies[(j + turn) % len(dies)]]
-        out.append(mine[(j // len(dies)) % len(mine)])
+        out.append(mine[(j // len(dies) + 2 * (turn // len(dies))) % len(mine)])
     return out
 
 
 def _unit(t, k):
     return t[k * 128:(k + 1) * 128, :]
+
+
+def _group(t, q):
+    return t[q * U * 128:(q + 1) * U * 128, :]
 
 
 def rank_program(g, core, T, topo):
@@ -64,36 +71,44 @@ def rank_program(g, core, T, topo):
             ids.append(DstId(rid=rid, pnc=pid))
         g.wait_ge(S.arr, NR)
         g.remote_dma_fused([RemoteDMATransfer(
-            dst_ids=ids, dma_engine_mask=sum(eng), remote_sem=S.got,
+            dst_ids=ids, dma_engine_mask=sum(eng), remote_sem=S["got%d" % (k // U)],
             srcs=[_unit(T.land, i) for i in range(NR)],
             dsts=[_unit(T.res, k) for _ in ranks], alu_op=1)], local_sem=S.snt)
         g.wait_ge(S.snt, len(eng))
         return
 
-    half = R * 128 // 2
-    g.sync.dma_start(T.src[0:half, :], T.a[:, :]).then_inc(S.ld, 16)
-    g.scalar.dma_start(T.src[half:2 * half, :], T.b[:, :]).then_inc(S.ld, 16)
+    queue = [g.sync, g.scalar]
+    tens = [T.a, T.b]
+    for q in range(G):
+        r0 = 64 * (q // 2)
+        queue[q % 2].dma_start(_group(T.src, q), tens[q % 2][r0:r0 + 64, :]).then_inc(S["ld%d" % q], 16)
     eng = _engines(topo, core, red)
-    g.wait_ge(S.ld, 32)
-    for k0 in range(0, R, len(eng)):
+    assert len(eng) >= U
+    for q in range(G):
         trs = []
-        for k in range(k0, min(R, k0 + len(eng))):
+        for u in range(U):
+            k = q * U + u
             rid, pid = topo.addr(red[k], core)
             trs.append(RemoteDMATransfer(
-                dst_ids=[DstId(rid=rid, pnc=pid)], dma_engine_mask=eng[k - k0], remote_sem=S.arr,
+                dst_ids=[DstId(rid=rid, pnc=pid)], dma_engine_mask=eng[u], remote_sem=S.arr,
                 src=_unit(T.src, k), dst=_unit(T.land, rank)))
+        g.wait_ge(S["ld%d" % q], 16)
         g.remote_dma_fused(trs, local_sem=S.snt)
 
-    total = sum(len(_engines(topo, h, ranks)) for h in red)
-    g.sync.wait_ge(S.got, total)
-    g.sync.dma_start(T.ab[:, 0:128], T.res[0:half, :]).then_inc(S.ld2, 16)
-    g.scalar.wait_ge(S.got, total)
-    g.scalar.dma_start(T.ab[:, 128:256], T.res[half:2 * half, :]).then_inc(S.ld2, 16)
-    g.tensor.wait_ge(S.ld2, 32)
-    g.tensor.matmul(T.ps[:, :], T.ab[:, 0:128], T.ab[:, 128:256], True, True).then_inc(S.mm, 1)
+    for q in range(G):
+        r0 = 64 * (q // 2)
+        c0 = 128 * (q % 2)
+        total = sum(len(_engines(topo, h, ranks)) for h in red[q * U:(q + 1) * U])
+        queue[q % 2].wait_ge(S["got%d" % q], total)
+        queue[q % 2].dma_start(T.ab[r0:r0 + 64, c0:c0 + 128], _group(T.res, q)).then_inc(S["lx%d" % (q // 2)], 16)
+    g.tensor.wait_ge(S.lx0, 32)
+    g.tensor.matmul(T.ps[:, :], T.ab[0:64, 0:128], T.ab[0:64, 128:256], True, False).then_inc(S.m1, 1)
+    g.tensor.wait_ge(S.lx1, 32)
+    g.tensor.wait_ge(S.m1, 1)
+    g.tensor.matmul(T.ps[:, :], T.ab[64:128, 0:128], T.ab[64:128, 128:256], False, True).then_inc(S.mm, 1)
     g.vector.wait_ge(S.mm, 1)
     g.vector.tensor_copy(T.ysb[:, :], T.ps[:, :]).then_inc(S.cp, 1)
     g.sync.wait_ge(S.cp, 1)
     g.sync.dma_start(T.y[:, :], T.ysb[:, :]).then_inc(S.st, 16)
     g.sync.wait_ge(S.st, 16)
-    g.wait_ge(S.snt, R)
+    g.wait_ge(S.snt, G * U)

from concourse.bass import DstId, RemoteDMATransfer

G = 4
NR = 9
GE = 2 * 128 * 128 // G

SEMAPHORES = (["ld%d" % q for q in range(G)] + ["got%d" % q for q in range(G)]
              + ["lx0", "lx1", "snt", "arr", "m1", "mm", "cp", "st"])
U = 8
UW = GE // U // 128
SCRATCH = {
    "src": ("dram", [G * U * 128, UW], "bfloat16"),
    "land": ("dram", [NR * 128, UW], "bfloat16"),
    "res": ("dram", [G * U * 128, UW], "bfloat16"),
    "ab": ("sbuf", [128, 256], "bfloat16"),
    "ysb": ("sbuf", [128, 128], "bfloat16"),
    "ps": ("psum", [128, 128], "float32"),
}


def _engines(topo, src, dsts):
    m = topo.mask(src, dsts[0])
    for d in dsts[1:]:
        m &= topo.mask(src, d)
    return [1 << i for i in range(m.bit_length()) if (m >> i) & 1]


def _reducers(T, topo):
    ranks = list(T.cores)
    per = topo.CORES_PER_HOST
    chips = {}
    for h in sorted(set(topo.host(r) for r in ranks)):
        for c in range(h * per, (h + 1) * per):
            if c in ranks:
                continue
            if all(topo.may_write(r, c) and topo.may_write(c, r) for r in ranks):
                chips.setdefault((topo.host(c), topo.chip(c)), []).append(c)
    keys = sorted(chips)
    out = []
    for k in range(G * U):
        j, turn = k % len(keys), k // len(keys)
        cs = chips[keys[j]]
        dies = sorted(set(topo.die(c) for c in cs))
        mine = [c for c in cs if topo.die(c) == dies[(j + turn) % len(dies)]]
        out.append(mine[(j // len(dies) + 2 * (turn // len(dies))) % len(mine)])
    return out


def _unit(t, k):
    return t[k * 128:(k + 1) * 128, :]


def _group(t, q):
    return t[q * U * 128:(q + 1) * U * 128, :]


def rank_program(g, core, T, topo):
    ranks = list(T.cores)
    red = _reducers(T, topo)
    rank = T.rank_of(core)
    S = T.sem

    if rank is None:
        if core not in red:
            return
        k = red.index(core)
        eng = _engines(topo, core, ranks)
        ids = []
        for r in ranks:
            rid, pid = topo.addr(r, core)
            ids.append(DstId(rid=rid, pnc=pid))
        g.wait_ge(S.arr, NR)
        g.remote_dma_fused([RemoteDMATransfer(
            dst_ids=ids, dma_engine_mask=sum(eng), remote_sem=S["got%d" % (k // U)],
            srcs=[_unit(T.land, i) for i in range(NR)],
            dsts=[_unit(T.res, k) for _ in ranks], alu_op=1)], local_sem=S.snt)
        g.wait_ge(S.snt, len(eng))
        return

    queue = [g.sync, g.scalar]
    tens = [T.a, T.b]
    for q in range(G):
        r0 = 64 * (q // 2)
        queue[q % 2].dma_start(_group(T.src, q), tens[q % 2][r0:r0 + 64, :]).then_inc(S["ld%d" % q], 16)
    eng = _engines(topo, core, red)
    assert len(eng) >= U
    for q in range(G):
        trs = []
        for u in range(U):
            k = q * U + u
            rid, pid = topo.addr(red[k], core)
            trs.append(RemoteDMATransfer(
                dst_ids=[DstId(rid=rid, pnc=pid)], dma_engine_mask=eng[u], remote_sem=S.arr,
                src=_unit(T.src, k), dst=_unit(T.land, rank)))
        g.wait_ge(S["ld%d" % q], 16)
        g.remote_dma_fused(trs, local_sem=S.snt)

    for q in range(G):
        r0 = 64 * (q // 2)
        c0 = 128 * (q % 2)
        total = sum(len(_engines(topo, h, ranks)) for h in red[q * U:(q + 1) * U])
        queue[q % 2].wait_ge(S["got%d" % q], total)
        queue[q % 2].dma_start(T.ab[r0:r0 + 64, c0:c0 + 128], _group(T.res, q)).then_inc(S["lx%d" % (q // 2)], 16)
    g.tensor.wait_ge(S.lx0, 32)
    g.tensor.matmul(T.ps[:, :], T.ab[0:64, 0:128], T.ab[0:64, 128:256], True, False).then_inc(S.m1, 1)
    g.tensor.wait_ge(S.lx1, 32)
    g.tensor.wait_ge(S.m1, 1)
    g.tensor.matmul(T.ps[:, :], T.ab[64:128, 0:128], T.ab[64:128, 128:256], False, True).then_inc(S.mm, 1)
    g.vector.wait_ge(S.mm, 1)
    g.vector.tensor_copy(T.ysb[:, :], T.ps[:, :]).then_inc(S.cp, 1)
    g.sync.wait_ge(S.cp, 1)
    g.sync.dma_start(T.y[:, :], T.ysb[:, :]).then_inc(S.st, 16)
    g.sync.wait_ge(S.st, 16)
    g.wait_ge(S.snt, G * U)
